import numpy as np
import ml_dtypes

BF16 = ml_dtypes.bfloat16


def bf(x):
    return np.asarray(x, np.float32).astype(BF16)


def f32(x):
    return np.asarray(x, np.float32)


def f64(x):
    return np.asarray(x).astype(np.float64)


def striped(idx):
    return np.tile(idx.reshape(-1, 16).T, (8, 1))


def rows(idx, k):
    return np.tile(idx, (k, 1))


def look(tab, idx):
    return np.take_along_axis(f64(tab), rows(idx, len(tab)), axis=1)


K, S, D, V, N, M = 256, 256, 4, 64, 256, 256


def setup_inputs():
    return {"tab": f32(np.random.standard_normal((K, S))), "x0": f32(np.random.standard_normal((K, V))), "w": bf(np.random.standard_normal((K, M)) / np.sqrt(K)), "b": f32(0.5 * np.random.standard_normal((M, 1))), "offs": striped(np.random.permutation(S)[:N])}


def reference(tab, x0, w, b, offs):
    idx = offs[:16].T.reshape(-1)
    x = f64(x0)
    for d in range(D):
        x = np.minimum(x, look(tab, idx[d * V:(d + 1) * V]))
    y = f64(w).T @ x
    return np.maximum(y + f64(b), 0.0)

@@ -1,0 +1,52 @@
+import concourse.mybir as mybir
+
+F32, BF16, U16 = mybir.dt.float32, mybir.dt.bfloat16, mybir.dt.uint16
+ALU = mybir.AluOpType
+
+P = 128
+K, S = 256, 256
+D, V, M = 4, 64, 256
+N = D * V
+RB, MB = K // P, M // P
+FLOPS = 2 * K * M * V
+
+
+def tile_lookup_pool_min_relu_kernel(tc, tab, x0, w, b, offs, out):
+    nc = tc.nc
+    with (
+        tc.tile_pool(name="held", bufs=1) as held,
+        tc.psum_pool(name="psum", bufs=1) as psum,
+    ):
+        tab_rows = tab.rearrange("(p k) s -> p k s", k=RB)
+        lists = held.tile([P, N // 16], U16, name="lists")
+        nc.sync.dma_start(lists[:], offs)
+        windows = [held.tile([P, S], F32, name=f"window{k}") for k in range(RB)]
+        centre = held.tile([P, RB, V], F32, name="centre")
+        nc.scalar.dma_start(centre[:], x0.rearrange("(p k) j -> p k j", k=RB))
+        nc.sync.dma_start(windows[0][:], tab_rows[:, 0, :])
+        nc.scalar.dma_start(windows[1][:], tab_rows[:, 1, :])
+        weights = held.tile([P, RB, M], BF16, name="weights")
+        nc.gpsimd.dma_start(weights[:], w.rearrange("(p k) m -> p k m", k=RB))
+        bias = held.tile([P, MB], F32, name="bias")
+        nc.gpsimd.dma_start(bias[:], b.rearrange("(p h) o -> p (h o)", h=MB))
+
+        operands = []
+        for k in range(RB):
+            smallest = centre[:, k, :]
+            for d in range(D):
+                piece = lists[:, d * (V // 16):(d + 1) * (V // 16)]
+                new = held.tile([P, V], F32, name=f"min{k}_{d}")
+                nc.vector.tensor_tensor(new[:], windows[k][:].indirect(piece), smallest, ALU.min)
+                smallest = new[:]
+            x = held.tile([P, V], BF16, name=f"x{k}")
+            nc.vector.tensor_copy(x[:], smallest)
+            operands.append(x)
+
+        sums = [psum.tile([P, V], F32, name=f"sum{h}") for h in range(MB)]
+        for k in range(RB):
+            for h in range(MB):
+                nc.tensor.matmul(sums[h][:], weights[:, k, h::MB], operands[k][:], start=k == 0, stop=k == RB - 1)
+        result = held.tile([P, MB, V], F32, name="result")
+        for h in range(MB):
+            nc.vector.tensor_scalar(result[:, h, :], sums[h][:], bias[:, h:h + 1], 0.0, op0=ALU.add, op1=ALU.max)
+        nc.sync.dma_start(out.rearrange("(p h) j -> p h j", h=MB), result[:])

@@ -26,9 +26,9 @@ def tile_lookup_pool_min_relu_kernel(tc, tab, x0, w, b, offs, out):
         nc.sync.dma_start(windows[0][:], tab_rows[:, 0, :])
         nc.scalar.dma_start(windows[1][:], tab_rows[:, 1, :])
         weights = held.tile([P, RB, M], BF16, name="weights")
-        nc.gpsimd.dma_start(weights[:], w.rearrange("(p k) m -> p k m", k=RB))
+        nc.sync.dma_start(weights[:], w.rearrange("(p k) m -> p k m", k=RB))
         bias = held.tile([P, MB], F32, name="bias")
-        nc.gpsimd.dma_start(bias[:], b.rearrange("(p h) o -> p (h o)", h=MB))
+        nc.scalar.dma_start(bias[:], b.rearrange("(p h) o -> p (h o)", h=MB))
 
         operands = []
         for k in range(RB):

@@ -32,14 +32,15 @@ def tile_lookup_pool_min_relu_kernel(tc, tab, x0, w, b, offs, out):
 
         operands = []
         for k in range(RB):
-            smallest = centre[:, k, :]
-            for d in range(D):
+            first = held.tile([P, 2 * V], F32, name=f"first{k}")
+            for d in range(2):
                 piece = lists[:, d * (V // 16):(d + 1) * (V // 16)]
-                new = held.tile([P, V], F32, name=f"min{k}_{d}")
-                nc.vector.tensor_tensor(new[:], windows[k][:].indirect(piece), smallest, ALU.min)
-                smallest = new[:]
+                half = first[:, d * V:(d + 1) * V]
+                nc.vector.tensor_tensor(half, windows[k][:].indirect(piece), centre[:, k, :], ALU.min)
+            both = held.tile([P, 2 * V], F32, name=f"both{k}")
+            nc.vector.tensor_tensor(both[:], windows[k][:].indirect(lists[:, 2 * V // 16:]), first[:], ALU.min)
             x = held.tile([P, V], BF16, name=f"x{k}")
-            nc.vector.tensor_copy(x[:], smallest)
+            nc.vector.tensor_tensor(x[:], both[:, 0:V], both[:, V:2 * V], ALU.min)
             operands.append(x)
 
         sums = [psum.tile([P, V], F32, name=f"sum{h}") for h in range(MB)]

@@ -30,18 +30,18 @@ def tile_lookup_pool_min_relu_kernel(tc, tab, x0, w, b, offs, out):
         bias = held.tile([P, MB], F32, name="bias")
         nc.scalar.dma_start(bias[:], b.rearrange("(p h) o -> p (h o)", h=MB))
 
-        operands = []
+        first = [held.tile([P, 2 * V], F32, name=f"first{k}") for k in range(RB)]
+        both = [held.tile([P, 2 * V], F32, name=f"both{k}") for k in range(RB)]
+        operands = [held.tile([P, V], BF16, name=f"x{k}") for k in range(RB)]
         for k in range(RB):
-            first = held.tile([P, 2 * V], F32, name=f"first{k}")
             for d in range(2):
                 piece = lists[:, d * (V // 16):(d + 1) * (V // 16)]
-                half = first[:, d * V:(d + 1) * V]
+                half = first[k][:, d * V:(d + 1) * V]
                 nc.vector.tensor_tensor(half, windows[k][:].indirect(piece), centre[:, k, :], ALU.min)
-            both = held.tile([P, 2 * V], F32, name=f"both{k}")
-            nc.vector.tensor_tensor(both[:], windows[k][:].indirect(lists[:, 2 * V // 16:]), first[:], ALU.min)
-            x = held.tile([P, V], BF16, name=f"x{k}")
-            nc.vector.tensor_tensor(x[:], both[:, 0:V], both[:, V:2 * V], ALU.min)
-            operands.append(x)
+        for k in range(RB):
+            nc.vector.tensor_tensor(both[k][:], windows[k][:].indirect(lists[:, 2 * V // 16:]), first[k][:], ALU.min)
+        for k in range(RB):
+            nc.vector.tensor_tensor(operands[k][:], both[k][:, 0:V], both[k][:, V:2 * V], ALU.min)
 
         sums = [psum.tile([P, V], F32, name=f"sum{h}") for h in range(MB)]
         for k in range(RB):

import concourse.mybir as mybir

F32, BF16, U16 = mybir.dt.float32, mybir.dt.bfloat16, mybir.dt.uint16
ALU = mybir.AluOpType

P = 128
K, S = 256, 256
D, V, M = 4, 64, 256
N = D * V
RB, MB = K // P, M // P
FLOPS = 2 * K * M * V


def tile_lookup_pool_min_relu_kernel(tc, tab, x0, w, b, offs, out):
    nc = tc.nc
    with (
        tc.tile_pool(name="held", bufs=1) as held,
        tc.psum_pool(name="psum", bufs=1) as psum,
    ):
        tab_rows = tab.rearrange("(p k) s -> p k s", k=RB)
        lists = held.tile([P, N // 16], U16, name="lists")
        nc.sync.dma_start(lists[:], offs)
        windows = [held.tile([P, S], F32, name=f"window{k}") for k in range(RB)]
        centre = held.tile([P, RB, V], F32, name="centre")
        nc.scalar.dma_start(centre[:], x0.rearrange("(p k) j -> p k j", k=RB))
        nc.sync.dma_start(windows[0][:], tab_rows[:, 0, :])
        nc.scalar.dma_start(windows[1][:], tab_rows[:, 1, :])
        weights = held.tile([P, RB, M], BF16, name="weights")
        nc.sync.dma_start(weights[:], w.rearrange("(p k) m -> p k m", k=RB))
        bias = held.tile([P, MB], F32, name="bias")
        nc.scalar.dma_start(bias[:], b.rearrange("(p h) o -> p (h o)", h=MB))

        first = [held.tile([P, 2 * V], F32, name=f"first{k}") for k in range(RB)]
        both = [held.tile([P, 2 * V], F32, name=f"both{k}") for k in range(RB)]
        operands = [held.tile([P, V], BF16, name=f"x{k}") for k in range(RB)]
        for k in range(RB):
            for d in range(2):
                piece = lists[:, d * (V // 16):(d + 1) * (V // 16)]
                half = first[k][:, d * V:(d + 1) * V]
                nc.vector.tensor_tensor(half, windows[k][:].indirect(piece), centre[:, k, :], ALU.min)
        for k in range(RB):
            nc.vector.tensor_tensor(both[k][:], windows[k][:].indirect(lists[:, 2 * V // 16:]), first[k][:], ALU.min)
        for k in range(RB):
            nc.vector.tensor_tensor(operands[k][:], both[k][:, 0:V], both[k][:, V:2 * V], ALU.min)

        sums = [psum.tile([P, V], F32, name=f"sum{h}") for h in range(MB)]
        for k in range(RB):
            for h in range(MB):
                nc.tensor.matmul(sums[h][:], weights[:, k, h::MB], operands[k][:], start=k == 0, stop=k == RB - 1)
        result = held.tile([P, MB, V], F32, name="result")
        for h in range(MB):
            nc.vector.tensor_scalar(result[:, h, :], sums[h][:], bias[:, h:h + 1], 0.0, op0=ALU.add, op1=ALU.max)
        nc.sync.dma_start(out.rearrange("(p h) j -> p h j", h=MB), result[:])
